import numpy as np, ml_dtypes
CORES = [10,34,74,98]
N = 4
R, TK = 32, 128
WID = [16,64,128,48]
def setup_inputs(rng):
    u = (rng.standard_normal((N, 128, R), dtype=np.float32) / 11).astype(ml_dtypes.bfloat16)
    return {"x": rng.standard_normal((N, 128, TK), dtype=np.float32).astype(ml_dtypes.bfloat16), "u": u, "ut": u.transpose(0, 2, 1).copy(), "vt": rng.standard_normal((N, R, 128), dtype=np.float32).astype(ml_dtypes.bfloat16)}
def setup_inputs_big(rng):
    d = setup_inputs(rng)
    for k in ("x", "u", "ut", "vt"): d[k] = (d[k].astype(np.float32) * 1024.0).astype(d[k].dtype)
    return d
def setup_inputs_small(rng):
    d = setup_inputs(rng)
    for k in ("x", "u", "ut", "vt"): d[k] = (d[k].astype(np.float32) * (1 / 1024.0)).astype(d[k].dtype)
    return d
def setup_inputs_apart(rng):
    d = setup_inputs(rng)
    f = (10.0 ** rng.permutation(np.linspace(-1.5, 1.5, N))).astype(np.float32).reshape(N, 1, 1)
    for k in ("x", "u", "ut", "vt"): d[k] = (d[k].astype(np.float32) * f).astype(d[k].dtype)
    return d
def tie_inputs(x):
    x = dict(x)
    x["ut"] = x["u"].transpose(0, 2, 1).copy()
    return x
def whole(x, u, ut, vt):
    X, U, VT = x.astype(np.float64), u.astype(np.float64), vt.astype(np.float64)
    y = np.stack([sum(VT[j].T @ (U[j].T @ X[r]) for j in range(N)) for r in range(N)])
    return {"y": y.astype(ml_dtypes.bfloat16 if x.dtype != np.float64 else np.float64)}
def reference(x, u, ut, vt):
    o = whole(x, u, ut, vt)["y"].copy()
    for r in range(N):
        o[r][:, WID[r]:] = np.nan
    return {"y": o}

@@ -1,0 +1,85 @@
+from concourse.bass import DstId, RemoteDMATransfer
+
+N = 4
+R = 32
+ENGINES = 4
+
+SCRATCH = {
+    "fac": ("dram", [N, 128, 64], "bfloat16"),
+    "utc": ("sbuf", [128, 128], "bfloat16"),
+    "vtc": ("sbuf", [128, 128], "bfloat16"),
+    "xs": ("sbuf", [128, 128], "bfloat16"),
+    "wsb": ("sbuf", [128, 128], "bfloat16"),
+    "ysb": ("sbuf", [128, 128], "bfloat16"),
+    "wps": ("psum", [128, 512], "float32"),
+    "yps": ("psum", [128, 512], "float32"),
+}
+SEMAPHORES = ["staged", "sent", "arr0", "arr1", "arr2", "arr3", "ready", "mm1", "cp1", "mm2", "cp2", "stored"]
+
+
+def _hops(topo, a, b):
+    ca, cb = topo.chip(a), topo.chip(b)
+    if ca == cb:
+        return 0
+    return 1 if (topo.mates(ca, cb) or topo.same_plane(ca, cb)) else 2
+
+
+def _engines(topo, core, peers, n):
+    common = topo.mask(core, peers[0])
+    for p in peers[1:]:
+        common &= topo.mask(core, p)
+    bits = [b for b in range(common.bit_length()) if (common >> b) & 1]
+    m = 0
+    for b in bits[::len(bits) // n][:n]:
+        m |= 1 << b
+    return m
+
+
+def rank_program(g, core, T, topo):
+    j = T.rank_of(core)
+    if j is None:
+        return
+    wid = T.tables["WID"][j]
+    peers = [c for c in T.cores if c != core]
+    for p in peers:
+        if not topo.may_write(core, p):
+            raise ValueError("rank cores must be able to write to one another")
+    sem = T.sem
+    own = slice(R * j, R * (j + 1))
+
+    g.sync.dma_start(out=T.fac[j, 0:64, :], in_=T.ut[:, :]).then_inc(sem.staged, 16)
+    g.scalar.dma_start(out=T.fac[j, 64:128, :], in_=T.vt[:, :]).then_inc(sem.staged, 16)
+    g.sync.dma_start(out=T.utc[own, :], in_=T.ut[:, :]).then_inc(sem.ready, 16)
+    g.scalar.dma_start(out=T.vtc[own, :], in_=T.vt[:, :]).then_inc(sem.ready, 16)
+    g.sync.dma_start(out=T.xs[:, 0:wid], in_=T.x[:, 0:wid]).then_inc(sem.ready, 16)
+
+    ids = []
+    for p in peers:
+        rid, pid, _ = topo.addr(p)
+        ids.append(DstId(rid=rid, pnc=pid))
+    g.wait_ge(sem.staged, 32)
+    g.remote_dma_fused(
+        [RemoteDMATransfer(dst_ids=ids, dma_engine_mask=_engines(topo, core, peers, ENGINES),
+                           remote_sem=sem["arr%d" % j], srcs=[T.fac[j]], dsts=[T.fac[j] for _ in peers], alu_op=0)],
+        local_sem=sem.sent)
+
+    for p in sorted(peers, key=lambda c: _hops(topo, c, core)):
+        s = T.rank_of(p)
+        rows = slice(R * s, R * (s + 1))
+        g.sync.wait_ge(sem["arr%d" % s], ENGINES)
+        g.sync.dma_start(out=T.utc[rows, :], in_=T.fac[s, 0:64, :]).then_inc(sem.ready, 16)
+        g.scalar.wait_ge(sem["arr%d" % s], ENGINES)
+        g.scalar.dma_start(out=T.vtc[rows, :], in_=T.fac[s, 64:128, :]).then_inc(sem.ready, 16)
+
+    g.tensor.wait_ge(sem.ready, 16 * (2 * N + 1))
+    g.tensor.matmul(T.wps[:, 0:128], T.utc[:, :], T.vtc[:, :], True, True).then_inc(sem.mm1, 1)
+    g.vector.wait_ge(sem.mm1, 1)
+    g.vector.tensor_copy(T.wsb[:, :], T.wps[:, 0:128]).then_inc(sem.cp1, 1)
+    g.tensor.wait_ge(sem.cp1, 1)
+    g.tensor.matmul(T.yps[:, 0:wid], T.wsb[:, :], T.xs[:, 0:wid], True, True).then_inc(sem.mm2, 1)
+    g.vector.wait_ge(sem.mm2, 1)
+    g.vector.tensor_copy(T.ysb[:, 0:wid], T.yps[:, 0:wid]).then_inc(sem.cp2, 1)
+    g.sync.wait_ge(sem.cp2, 1)
+    g.sync.dma_start(out=T.y[:, 0:wid], in_=T.ysb[:, 0:wid]).then_inc(sem.stored, 16)
+    g.sync.wait_ge(sem.stored, 16)
+    g.wait_ge(sem.sent, ENGINES)

@@ -2,19 +2,22 @@ from concourse.bass import DstId, RemoteDMATransfer
 
 N = 4
 R = 32
-ENGINES = 4
+EV = 4
+EU = 8
 
 SCRATCH = {
-    "fac": ("dram", [N, 128, 64], "bfloat16"),
-    "utc": ("sbuf", [128, 128], "bfloat16"),
+    "fv": ("dram", [N, 128, 32], "bfloat16"),
+    "fu": ("dram", [128, 32], "bfloat16"),
+    "ucat": ("sbuf", [128, 128], "bfloat16"),
     "vtc": ("sbuf", [128, 128], "bfloat16"),
     "xs": ("sbuf", [128, 128], "bfloat16"),
-    "wsb": ("sbuf", [128, 128], "bfloat16"),
+    "tsb": ("sbuf", [128, 128], "bfloat16"),
     "ysb": ("sbuf", [128, 128], "bfloat16"),
-    "wps": ("psum", [128, 512], "float32"),
+    "tps": ("psum", [128, 512], "float32"),
     "yps": ("psum", [128, 512], "float32"),
 }
-SEMAPHORES = ["staged", "sent", "arr0", "arr1", "arr2", "arr3", "ready", "mm1", "cp1", "mm2", "cp2", "stored"]
+SEMAPHORES = ["stv", "stu", "sent", "arr0", "arr1", "arr2", "arr3", "uarr", "local", "vready",
+              "mm1", "cp1", "mm2", "cp2", "stored"]
 
 
 def _hops(topo, a, b):
@@ -47,39 +50,46 @@ def rank_program(g, core, T, topo):
     sem = T.sem
     own = slice(R * j, R * (j + 1))
 
-    g.sync.dma_start(out=T.fac[j, 0:64, :], in_=T.ut[:, :]).then_inc(sem.staged, 16)
-    g.scalar.dma_start(out=T.fac[j, 64:128, :], in_=T.vt[:, :]).then_inc(sem.staged, 16)
-    g.sync.dma_start(out=T.utc[own, :], in_=T.ut[:, :]).then_inc(sem.ready, 16)
-    g.scalar.dma_start(out=T.vtc[own, :], in_=T.vt[:, :]).then_inc(sem.ready, 16)
-    g.sync.dma_start(out=T.xs[:, 0:wid], in_=T.x[:, 0:wid]).then_inc(sem.ready, 16)
+    g.sync.dma_start(out=T.fv[j], in_=T.vt[:, :]).then_inc(sem.stv, 16)
+    g.scalar.dma_start(out=T.fu[:, :], in_=T.u[:, :]).then_inc(sem.stu, 16)
+    g.sync.dma_start(out=T.vtc[own, :], in_=T.vt[:, :]).then_inc(sem.vready, 16)
+    g.scalar.dma_start(out=T.ucat[:, own], in_=T.u[:, :]).then_inc(sem.local, 16)
+    g.sync.dma_start(out=T.xs[:, 0:wid], in_=T.x[:, 0:wid]).then_inc(sem.local, 16)
 
     ids = []
     for p in peers:
         rid, pid, _ = topo.addr(p)
         ids.append(DstId(rid=rid, pnc=pid))
-    g.wait_ge(sem.staged, 32)
+    g.wait_ge(sem.stv, 16)
     g.remote_dma_fused(
-        [RemoteDMATransfer(dst_ids=ids, dma_engine_mask=_engines(topo, core, peers, ENGINES),
-                           remote_sem=sem["arr%d" % j], srcs=[T.fac[j]], dsts=[T.fac[j] for _ in peers], alu_op=0)],
+        [RemoteDMATransfer(dst_ids=ids, dma_engine_mask=_engines(topo, core, peers, EV),
+                           remote_sem=sem["arr%d" % j], srcs=[T.fv[j]], dsts=[T.fv[j] for _ in peers], alu_op=0)],
+        local_sem=sem.sent)
+    g.wait_ge(sem.stu, 16)
+    g.remote_dma_fused(
+        [RemoteDMATransfer(dst_ids=ids, dma_engine_mask=_engines(topo, core, peers, EU),
+                           remote_sem=sem.uarr, srcs=[T.fu[:, :]], dsts=[T.ucat[:, own] for _ in peers], alu_op=0)],
         local_sem=sem.sent)
 
-    for p in sorted(peers, key=lambda c: _hops(topo, c, core)):
+    queues = [g.scalar, g.sync]
+    for i, p in enumerate(sorted(peers, key=lambda c: _hops(topo, c, core))):
         s = T.rank_of(p)
-        rows = slice(R * s, R * (s + 1))
-        g.sync.wait_ge(sem["arr%d" % s], ENGINES)
-        g.sync.dma_start(out=T.utc[rows, :], in_=T.fac[s, 0:64, :]).then_inc(sem.ready, 16)
-        g.scalar.wait_ge(sem["arr%d" % s], ENGINES)
-        g.scalar.dma_start(out=T.vtc[rows, :], in_=T.fac[s, 64:128, :]).then_inc(sem.ready, 16)
+        q = queues[i % 2]
+        q.wait_ge(sem["arr%d" % s], EV)
+        q.dma_start(out=T.vtc[R * s:R * (s + 1), :], in_=T.fv[s]).then_inc(sem.vready, 16)
 
-    g.tensor.wait_ge(sem.ready, 16 * (2 * N + 1))
-    g.tensor.matmul(T.wps[:, 0:128], T.utc[:, :], T.vtc[:, :], True, True).then_inc(sem.mm1, 1)
+    g.tensor.wait_ge(sem.local, 32)
+    g.tensor.wait_ge(sem.uarr, EU * len(peers))
+    g.tensor.matmul(T.tps[:, 0:wid], T.ucat[:, :], T.xs[:, 0:wid], True, True).then_inc(sem.mm1, 1)
     g.vector.wait_ge(sem.mm1, 1)
-    g.vector.tensor_copy(T.wsb[:, :], T.wps[:, 0:128]).then_inc(sem.cp1, 1)
+    g.vector.tensor_copy(T.tsb[:, 0:wid], T.tps[:, 0:wid]).then_inc(sem.cp1, 1)
+
     g.tensor.wait_ge(sem.cp1, 1)
-    g.tensor.matmul(T.yps[:, 0:wid], T.wsb[:, :], T.xs[:, 0:wid], True, True).then_inc(sem.mm2, 1)
+    g.tensor.wait_ge(sem.vready, 16 * N)
+    g.tensor.matmul(T.yps[:, 0:wid], T.vtc[:, :], T.tsb[:, 0:wid], True, True).then_inc(sem.mm2, 1)
     g.vector.wait_ge(sem.mm2, 1)
     g.vector.tensor_copy(T.ysb[:, 0:wid], T.yps[:, 0:wid]).then_inc(sem.cp2, 1)
     g.sync.wait_ge(sem.cp2, 1)
     g.sync.dma_start(out=T.y[:, 0:wid], in_=T.ysb[:, 0:wid]).then_inc(sem.stored, 16)
     g.sync.wait_ge(sem.stored, 16)
-    g.wait_ge(sem.sent, ENGINES)
+    g.wait_ge(sem.sent, EV + EU)

from concourse.bass import DstId, RemoteDMATransfer

N = 4
R = 32
EV = 4
EU = 8

SCRATCH = {
    "fv": ("dram", [N, 128, 32], "bfloat16"),
    "fu": ("dram", [128, 32], "bfloat16"),
    "ucat": ("sbuf", [128, 128], "bfloat16"),
    "vtc": ("sbuf", [128, 128], "bfloat16"),
    "xs": ("sbuf", [128, 128], "bfloat16"),
    "tsb": ("sbuf", [128, 128], "bfloat16"),
    "ysb": ("sbuf", [128, 128], "bfloat16"),
    "tps": ("psum", [128, 512], "float32"),
    "yps": ("psum", [128, 512], "float32"),
}
SEMAPHORES = ["stv", "stu", "sent", "arr0", "arr1", "arr2", "arr3", "uarr", "local", "vready",
              "mm1", "cp1", "mm2", "cp2", "stored"]


def _hops(topo, a, b):
    ca, cb = topo.chip(a), topo.chip(b)
    if ca == cb:
        return 0
    return 1 if (topo.mates(ca, cb) or topo.same_plane(ca, cb)) else 2


def _engines(topo, core, peers, n):
    common = topo.mask(core, peers[0])
    for p in peers[1:]:
        common &= topo.mask(core, p)
    bits = [b for b in range(common.bit_length()) if (common >> b) & 1]
    m = 0
    for b in bits[::len(bits) // n][:n]:
        m |= 1 << b
    return m


def rank_program(g, core, T, topo):
    j = T.rank_of(core)
    if j is None:
        return
    wid = T.tables["WID"][j]
    peers = [c for c in T.cores if c != core]
    for p in peers:
        if not topo.may_write(core, p):
            raise ValueError("rank cores must be able to write to one another")
    sem = T.sem
    own = slice(R * j, R * (j + 1))

    g.sync.dma_start(out=T.fv[j], in_=T.vt[:, :]).then_inc(sem.stv, 16)
    g.scalar.dma_start(out=T.fu[:, :], in_=T.u[:, :]).then_inc(sem.stu, 16)
    g.sync.dma_start(out=T.vtc[own, :], in_=T.vt[:, :]).then_inc(sem.vready, 16)
    g.scalar.dma_start(out=T.ucat[:, own], in_=T.u[:, :]).then_inc(sem.local, 16)
    g.sync.dma_start(out=T.xs[:, 0:wid], in_=T.x[:, 0:wid]).then_inc(sem.local, 16)

    ids = []
    for p in peers:
        rid, pid, _ = topo.addr(p)
        ids.append(DstId(rid=rid, pnc=pid))
    g.wait_ge(sem.stv, 16)
    g.remote_dma_fused(
        [RemoteDMATransfer(dst_ids=ids, dma_engine_mask=_engines(topo, core, peers, EV),
                           remote_sem=sem["arr%d" % j], srcs=[T.fv[j]], dsts=[T.fv[j] for _ in peers], alu_op=0)],
        local_sem=sem.sent)
    g.wait_ge(sem.stu, 16)
    g.remote_dma_fused(
        [RemoteDMATransfer(dst_ids=ids, dma_engine_mask=_engines(topo, core, peers, EU),
                           remote_sem=sem.uarr, srcs=[T.fu[:, :]], dsts=[T.ucat[:, own] for _ in peers], alu_op=0)],
        local_sem=sem.sent)

    queues = [g.scalar, g.sync]
    for i, p in enumerate(sorted(peers, key=lambda c: _hops(topo, c, core))):
        s = T.rank_of(p)
        q = queues[i % 2]
        q.wait_ge(sem["arr%d" % s], EV)
        q.dma_start(out=T.vtc[R * s:R * (s + 1), :], in_=T.fv[s]).then_inc(sem.vready, 16)

    g.tensor.wait_ge(sem.local, 32)
    g.tensor.wait_ge(sem.uarr, EU * len(peers))
    g.tensor.matmul(T.tps[:, 0:wid], T.ucat[:, :], T.xs[:, 0:wid], True, True).then_inc(sem.mm1, 1)
    g.vector.wait_ge(sem.mm1, 1)
    g.vector.tensor_copy(T.tsb[:, 0:wid], T.tps[:, 0:wid]).then_inc(sem.cp1, 1)

    g.tensor.wait_ge(sem.cp1, 1)
    g.tensor.wait_ge(sem.vready, 16 * N)
    g.tensor.matmul(T.yps[:, 0:wid], T.vtc[:, :], T.tsb[:, 0:wid], True, True).then_inc(sem.mm2, 1)
    g.vector.wait_ge(sem.mm2, 1)
    g.vector.tensor_copy(T.ysb[:, 0:wid], T.yps[:, 0:wid]).then_inc(sem.cp2, 1)
    g.sync.wait_ge(sem.cp2, 1)
    g.sync.dma_start(out=T.y[:, 0:wid], in_=T.ysb[:, 0:wid]).then_inc(sem.stored, 16)
    g.sync.wait_ge(sem.stored, 16)
    g.wait_ge(sem.sent, EV + EU)
